import numpy as np
import ml_dtypes


def mxq(x, axis, fmt="e4m3"):
    dtype, down = {"e4m3": (ml_dtypes.float8_e4m3fn, 7), "e5m2": (ml_dtypes.float8_e5m2, 14)}[fmt]
    v = np.moveaxis(np.asarray(x, np.float32).astype(ml_dtypes.bfloat16).astype(np.float64), axis, -1)
    blocks = v.reshape(v.shape[:-1] + (-1, 32))
    amax = np.abs(blocks).max(-1, keepdims=True)
    byte = np.maximum(np.where(amax > 0, np.frexp(amax)[1] - 1 + 127, 0) - down, 1)
    scale = np.exp2(byte - 127.0)
    codes = (blocks / scale).astype(np.float32).astype(dtype).astype(np.float64)
    return np.moveaxis((codes * scale).reshape(v.shape), -1, axis)


WIDE = False


def mx_kscale(k):
    if not WIDE:
        return np.ones(k)
    levels = np.array([10, -10, 5, -5, 0])
    if k % 512:
        return np.exp2(np.random.permutation(np.resize(levels, k // 32))).repeat(32)
    a = np.empty((k // 512, 16))
    for p in range(k // 512):
        a[p, :8] = np.random.permutation(np.resize(levels, 8))
        for g in range(8):
            far = levels[np.abs(levels - a[p, g]) >= 10]
            a[p, g + 8] = far[np.random.randint(len(far))]
    return np.exp2(a.ravel()).repeat(32)


def f64(x):
    return np.asarray(x).astype(np.float64)


def striped(idx):
    return np.tile(idx.reshape(-1, 16).T, (8, 1)).astype(np.uint16)


def unstriped(offs):
    return offs[:16].T.reshape(-1).astype(np.int64)


def pack_weight(w):
    k, n = w.shape
    w = f64(np.asarray(w, np.float32).astype(ml_dtypes.bfloat16)).reshape(k // 32, 32, n)
    amax = np.abs(w).max(1)
    byte = np.clip(np.where(amax > 0, np.frexp(amax)[1] - 1 + 127 - 7, 1), 1, 254)
    scaled = (w * np.exp2(127.0 - byte)[:, None, :]).reshape(k, n).astype(np.float32)
    words = np.ascontiguousarray(scaled.reshape(k // 512, 128, 4, n).transpose(0, 1, 3, 2)).astype(ml_dtypes.float8_e4m3fn).view(np.uint8)
    return words, np.ascontiguousarray(byte.astype(np.uint8).reshape(k // 512, 16, n))


def unpack_weight(words, scales):
    g, p, n, _ = words.shape
    vals = np.ascontiguousarray(words).view(ml_dtypes.float8_e4m3fn).astype(np.float64) * np.repeat(np.exp2(scales.astype(np.float64) - 127.0), 8, axis=1)[..., None]
    return vals.transpose(0, 1, 3, 2).reshape(g * 512, n)


def sigmoid(v):
    return 1.0 / (1.0 + np.exp(-np.maximum(v, -700.0)))


K, T, S, N, D = 512, 2048, 512, 256, 3
P = 2 ** 7


def setup_inputs():
    n = np.random.standard_normal
    s = mx_kscale(K)[:, None]
    packed_xT = pack_weight(n((K, T)) * s)
    return {
        "x_words": packed_xT[0],
        "x_scales": packed_xT[1],
        "w1": (n((K, N)) / np.sqrt(K) / s).astype(np.float32),
        "gain": (np.tile(np.random.uniform(0.05, 0.6, (D, 1, S)), (1, P, 1))).astype(np.float32),
        "hh": (np.tile(np.random.uniform(0.6, 1.6, S), (P, 1))).astype(np.float32),
        "noise": (np.random.uniform(0.05, 0.4, (N, 1))).astype(np.float32),
        "pri": (np.tile(np.random.uniform(0.5, 1.5, S), (P, 1))).astype(np.float32),
        "offs": striped(np.random.permutation(T)[:S]),
        "pos1": striped(np.random.permutation(S)[:S]),
        "pos2": striped(np.random.permutation(S)[:S]),
        "pos3": striped(np.random.permutation(S)[:S]),
    }


def reference(x_words, x_scales, w1, gain, hh, noise, pri, offs, pos1, pos2, pos3):
    xq = unpack_weight(x_words, x_scales)[:, unstriped(offs)]
    y = mxq(f64(w1), 0, "e4m3").T @ xq
    pp = sigmoid(y)
    bf = np.sqrt(pp)
    den = ((f64(hh)[:1]) ** 2) * pp + pp[:, unstriped(pos1)] * f64(gain)[0, :1] + pp[:, unstriped(pos2)] * f64(gain)[1, :1] + pp[:, unstriped(pos3)] * f64(gain)[2, :1] + f64(noise)
    ru = (f64(hh)[:1] * bf) / den
    mw = f64(pri)[:1] / (-1.0 * ((ru * f64(hh)[:1]) * bf) + 1.0)
    uw = mw * ((ru) ** 2)
    return ((mw * ru) * f64(hh)[:1]) / (((f64(hh)[:1]) ** 2) * uw + uw[:, unstriped(pos1)] * f64(gain)[0, :1] + uw[:, unstriped(pos2)] * f64(gain)[1, :1] + uw[:, unstriped(pos3)] * f64(gain)[2, :1] + 0.3)

@@ -1,0 +1,239 @@
+from contextlib import ExitStack
+
+import concourse.mybir as mybir
+from concourse.masks import make_identity
+
+K, T, S, N, D = 512, 2048, 512, 256, 3
+P = 128
+PACK = 4
+BLOCKS = N // P
+TILES = S // P
+HALF = S // 2
+SPARE = 16
+FLOPS = 2 * K * N * S
+
+F32 = mybir.dt.float32
+BF16 = mybir.dt.bfloat16
+I32 = mybir.dt.int32
+U32 = mybir.dt.uint32
+U16 = mybir.dt.uint16
+U8 = mybir.dt.uint8
+FP8X4 = mybir.dt.float8_e4m3fn_x4
+ALU = mybir.AluOpType
+ACT = mybir.ActivationFunctionType
+
+
+def tile_picked_ywmmse_tx_p_kernel(tc, x_words, x_scales, w1, gain, hh, noise, pri, offs, pos1, pos2, pos3, out):
+    nc = tc.nc
+    with ExitStack() as ctx:
+        lists = ctx.enter_context(tc.tile_pool(name="lists", bufs=1))
+        keep = ctx.enter_context(tc.tile_pool(name="keep", bufs=1))
+        ring = ctx.enter_context(tc.tile_pool(name="ring", bufs=4))
+        psum = ctx.enter_context(tc.psum_pool(name="psum", bufs=1))
+
+        def bank(index, name, tiles=TILES):
+            return psum.tile([P, tiles, P], F32, name=name, tag="bank%d" % index)
+
+        def flat(tile):
+            return tile[:].rearrange("p t c -> p (t c)")
+
+        rows = keep.tile([P, P], F32, name="rows")
+        nc.scalar.dma_start(rows[0:64, :], hh[0:16, :].rearrange("r (t c) -> (r t) c", c=P))
+        nc.scalar.dma_start(rows[64:128, :], pri[0:16, :].rearrange("r (t c) -> (r t) c", c=P))
+        xs_all = keep.tile([P, T], U8, name="xs_all")
+        nc.vector.memset(xs_all[:].bitcast(I32), 0)
+        ident = keep.tile([P, P], F32, name="ident")
+        make_identity(nc, ident[:])
+        noise_sb = keep.tile([P, BLOCKS, 1], F32, name="noise_sb")
+        with nc.allow_non_contiguous_dma(reason="one noise value a partition and block"):
+            nc.scalar.dma_start(noise_sb[:], noise.rearrange("(b p) o -> p b o", p=P))
+        power = [keep.tile([P, S + SPARE], F32, name="power%d" % b) for b in range(BLOCKS)]
+        weighted = [keep.tile([P, S + SPARE], F32, name="weighted%d" % b) for b in range(BLOCKS)]
+        for window in power + weighted:
+            nc.vector.memset(window[:, S:], 0.0)
+
+        offs_sb = lists.tile([P, S // 16], U16, name="offs_sb")
+        pos_sb = [lists.tile([P, S // 16], U16, name="pos_sb%d" % d) for d in range(D)]
+        nc.sync.dma_start(offs_sb[:], offs)
+        nc.sync.dma_start(pos_sb[0][:], pos1)
+        for q in range(4):
+            nc.scalar.dma_start(
+                xs_all[32 * q : 32 * q + 4, :].bitcast(I32), x_scales[0, 4 * q : 4 * q + 4, :].bitcast(I32)
+            )
+        w_rows = w1.rearrange("(p t) n -> p t n", t=PACK)
+        w_raw = [keep.tile([P, PACK, P], F32, name="w_raw%d" % b, tag="staged%d" % b) for b in range(BLOCKS)]
+        xw_all = keep.tile([P, T], U32, name="xw_all")
+        nc.sync.dma_start(w_raw[0][:], w_rows[:, :, 0:P])
+        nc.sync.dma_start(xw_all[:].bitcast(I32), x_words[0].rearrange("p n t -> p (n t)").bitcast(I32))
+        nc.sync.dma_start(w_raw[1][:], w_rows[:, :, P : 2 * P])
+        nc.sync.dma_start(pos_sb[1][:], pos2)
+        nc.sync.dma_start(pos_sb[2][:], pos3)
+
+        w_codes = []
+        w_scales = []
+
+        def quantise(b):
+            grouped = keep.tile([P, P, PACK], BF16, name="grouped%d" % b, tag="grouped%d" % b, align_bytes=64)
+            nc.vector.tensor_copy(
+                grouped[:].rearrange("p (c i) t -> p c t i", i=4),
+                w_raw[b][:].rearrange("p t (c i) -> p c t i", i=4),
+            )
+            w_codes.append(keep.tile([P, P], U32, name="w_codes%d" % b, align_bytes=64))
+            w_scales.append(keep.tile([P, P], U8, name="w_scales%d" % b, align_bytes=64))
+            nc.vector.quantize_mx(
+                out=w_codes[b][:].bitcast(FP8X4),
+                scales=w_scales[b][:],
+                in_=grouped[:].rearrange("p c t -> p (c t)"),
+            )
+
+        quantise(0)
+        gain_first = keep.tile([P, S], F32, name="gain_first", tag="staged0")
+        gain_rest = keep.tile([P, D - 1, S], F32, name="gain_rest", tag="grouped0", align_bytes=64)
+        nc.sync.dma_start(gain_first[:], gain[0])
+        nc.sync.dma_start(gain_rest[:], gain[1:D].rearrange("d p s -> p d s"))
+        gain_sb = [gain_first[:]] + [gain_rest[:, d, :] for d in range(D - 1)]
+
+        xs = keep.tile([P, S], U8, name="xs", align_bytes=64)
+        xw = keep.tile([P, S], U32, name="xw", align_bytes=64)
+        nc.vector.tensor_copy(xs[:], xs_all[:].indirect(offs_sb[:]))
+
+        turned = bank(5, "turned", 1)
+        nc.tensor.transpose(turned[:, 0, :], rows[:], ident[:])
+        h_abs = keep.tile([P, TILES], F32, name="h_abs")
+        nc.scalar.activation(h_abs[:], turned[:, 0, 0:TILES], ACT.Abs)
+        pri_col = keep.tile([P, TILES], F32, name="pri_col")
+        nc.scalar.copy(pri_col[:], turned[:, 0, 64 : 64 + TILES])
+        pri_h = keep.tile([P, TILES], F32, name="pri_h")
+        nc.vector.scalar_tensor_tensor(pri_h[:], h_abs[:], 1e-10, pri_col[:], ALU.max, ALU.mult)
+        pri_pos = keep.tile([P, TILES], F32, name="pri_pos")
+        nc.vector.tensor_scalar(pri_pos[:], pri_col[:], 1e-30, None, ALU.max)
+        pri_hh = keep.tile([P, TILES], F32, name="pri_hh")
+        nc.vector.tensor_tensor(pri_hh[:], pri_h[:], h_abs[:], ALU.mult)
+        inv_pri = keep.tile([P, TILES], F32, name="inv_pri")
+        nc.vector.reciprocal(inv_pri[:], pri_pos[:])
+        pri_hh_sq = keep.tile([P, TILES], F32, name="pri_hh_sq")
+        nc.scalar.activation(pri_hh_sq[:], pri_hh[:], ACT.Square)
+
+        def add_turned(into, term, first, last):
+            for place, (target, slot, t) in enumerate(into):
+                opens = place == 0 or into[place - 1][0] is not target
+                closes = place == len(into) - 1 or into[place + 1][0] is not target
+                nc.tensor.matmul(
+                    target[:, slot, :], term(t), ident[:], is_transpose=True,
+                    start=first and opens, stop=last and closes,
+                )
+
+        def whole(target):
+            return [(target, t, t) for t in range(TILES)]
+
+        heard = [bank(b, "heard%d" % b) for b in range(BLOCKS)]
+
+        def add_noise(b):
+            add_turned(whole(heard[b]), lambda t: noise_sb[:, b, :].to_broadcast([P, P]), False, False)
+
+        def product(b, index, lo, hi):
+            y = bank(index, "y", (hi - lo) // P)
+            nc.tensor.matmul_mx(
+                out=flat(y), lhsT=w_codes[b][:].bitcast(FP8X4), lhsT_scale=w_scales[b][:],
+                rhs=xw[:, lo:hi].bitcast(FP8X4), rhs_scale=xs[:, lo:hi], start=True, stop=True,
+            )
+            nc.scalar.activation(power[b][:, lo:hi], flat(y), ACT.Sigmoid)
+
+        for half in range(2):
+            lo, hi = half * HALF, (half + 1) * HALF
+            nc.vector.tensor_copy(xw[:, lo:hi], xw_all[:].indirect(offs_sb[:, lo // 16 : hi // 16]))
+            product(0, 2 + half, lo, hi)
+        quantise(1)
+        product(1, 4, 0, S)
+        hh_sb = keep.tile([P, S], F32, name="hh_sb", tag="staged1")
+        nc.sync.dma_start(hh_sb[:], hh)
+
+        inv_amp = []
+        for b in range(BLOCKS):
+            power_t = bank(5 + b, "power_t")
+            for t in range(TILES):
+                nc.tensor.transpose(power_t[:, t, :], power[b][:, t * P : (t + 1) * P], ident[:])
+            inv_amp.append(keep.tile([P, TILES, P], F32, name="inv_amp%d" % b, tag="inv_amp%d" % b))
+            for t in range(TILES):
+                nc.scalar.activation(
+                    inv_amp[b][:, t, :], power_t[:, t, :], ACT.Abs_reciprocal_sqrt,
+                    bias=1e-30, scale=pri_hh_sq[:, t : t + 1],
+                )
+        own = keep.tile([P, S], F32, name="own")
+        nc.scalar.activation(own[:], hh_sb[:], ACT.Square)
+
+        def neighbour(into, window, d, tag=None, first=False):
+            lo, hi = into[0][2] * P, (into[-1][2] + 1) * P
+            if tag is None:
+                term = ring.tile([P, hi - lo], F32, name="term")
+            else:
+                term = keep.tile([P, hi - lo], F32, name="term", tag=tag)
+            nc.vector.tensor_tensor(
+                term[:], window[:].indirect(pos_sb[d][:, lo // 16 : hi // 16]), gain_sb[d][:, lo:hi], ALU.mult
+            )
+            add_turned(into, lambda t: term[:, t * P - lo : (t + 1) * P - lo], first, d == D - 1)
+
+        scaled = [keep.tile([P, TILES, P], F32, name="scaled%d" % b, tag="scaled%d" % b) for b in range(BLOCKS)]
+        squared = [keep.tile([P, TILES, P], F32, name="squared%d" % b, tag="squared%d" % b) for b in range(BLOCKS)]
+
+        def scale_heard(b):
+            nc.vector.tensor_tensor(scaled[b][:], heard[b][:], inv_amp[b][:], ALU.mult)
+            for t in range(TILES):
+                nc.scalar.activation(squared[b][:, t, :], scaled[b][:, t, :], ACT.Square, scale=pri_h[:, t : t + 1])
+
+        def weigh(b):
+            total = keep.tile([P, TILES, P], F32, name="total%d" % b)
+            nc.vector.tensor_tensor(total[:], squared[b][:], heard[b][:], ALU.add)
+            root = keep.tile([P, TILES, P], F32, name="root%d" % b)
+            back = bank(2 + b, "back")
+            for t in range(TILES):
+                nc.scalar.activation(root[:, t, :], total[:, t, :], ACT.Abs_reciprocal_sqrt, scale=inv_pri[:, t : t + 1])
+                nc.tensor.transpose(back[:, t, :], root[:, t, :], ident[:])
+            nc.scalar.activation(weighted[b][:, :S], flat(back), ACT.Square)
+
+        def own_term(b, into):
+            term = ring.tile([P, S], F32, name="term")
+            nc.vector.tensor_tensor(term[:], weighted[b][:, :S], own[:], ALU.mult)
+            add_turned(into, lambda t: term[:, t * P : (t + 1) * P], True, False)
+
+        def finish(b, sums, first, count, index):
+            denom = keep.tile([P, count, P], F32, name="denom%d" % index)
+            nc.vector.scalar_tensor_tensor(
+                denom[:], sums[:], 0.3, scaled[b][:, first : first + count, :], ALU.add, ALU.mult
+            )
+            root = keep.tile([P, count, P], F32, name="root_out%d" % index)
+            nc.scalar.activation(root[:], denom[:], ACT.Abs_reciprocal_sqrt)
+            back = bank(index, "back_out", count)
+            for t in range(count):
+                nc.tensor.transpose(back[:, t, :], root[:, t, :], ident[:])
+            result = keep.tile([P, count * P], F32, name="result%d" % index)
+            nc.scalar.activation(result[:], flat(back), ACT.Square)
+            nc.sync.dma_start(out[b * P : (b + 1) * P, first * P : (first + count) * P], result[:])
+
+        neighbour(whole(heard[0]), power[0], 0, first=True)
+        add_noise(0)
+        for d in range(1, D):
+            neighbour(whole(heard[0]), power[0], d)
+        neighbour(whole(heard[1]), power[1], 0, first=True)
+        add_noise(1)
+        scale_heard(0)
+        neighbour(whole(heard[1]), power[1], 1, "inv_amp0")
+        weigh(0)
+        neighbour(whole(heard[1]), power[1], 2, "squared0")
+        scale_heard(1)
+        sums = bank(4, "sums")
+        own_term(0, whole(sums))
+        neighbour(whole(sums), weighted[0], 0)
+        weigh(1)
+        neighbour(whole(sums), weighted[0], 1, "squared1")
+        neighbour(whole(sums), weighted[0], 2)
+        halves = [bank(h, "sums_half", 2) for h in range(2)]
+        split = [(halves[t // 2], t % 2, t) for t in range(TILES)]
+        own_term(1, split)
+        neighbour(split, weighted[1], 0)
+        finish(0, sums, 0, TILES, 2)
+        neighbour(split, weighted[1], 1, "scaled0")
+        neighbour(split[:2], weighted[1], 2)
+        neighbour(split[2:], weighted[1], 2)
+        finish(1, halves[0], 0, 2, 3)
+        finish(1, halves[1], 2, 2, 5)

@@ -1,7 +1,6 @@
 from contextlib import ExitStack
 
 import concourse.mybir as mybir
-from concourse.masks import make_identity
 
 K, T, S, N, D = 512, 2048, 512, 256, 3
 P = 128
@@ -10,6 +9,7 @@ BLOCKS = N // P
 TILES = S // P
 HALF = S // 2
 SPARE = 16
+QUAD = 32
 FLOPS = 2 * K * N * S
 
 F32 = mybir.dt.float32
@@ -37,48 +37,56 @@ def tile_picked_ywmmse_tx_p_kernel(tc, x_words, x_scales, w1, gain, hh, noise, p
         def flat(tile):
             return tile[:].rearrange("p t c -> p (t c)")
 
-        rows = keep.tile([P, P], F32, name="rows")
-        nc.scalar.dma_start(rows[0:64, :], hh[0:16, :].rearrange("r (t c) -> (r t) c", c=P))
-        nc.scalar.dma_start(rows[64:128, :], pri[0:16, :].rearrange("r (t c) -> (r t) c", c=P))
         xs_all = keep.tile([P, T], U8, name="xs_all")
-        nc.vector.memset(xs_all[:].bitcast(I32), 0)
+        nc.gpsimd.memset(xs_all[:].bitcast(I32), 0)
+        ones = keep.tile([P, QUAD], F32, name="ones", tag="words", align_bytes=64)
+        nc.gpsimd.memset(ones[:], 1.0)
+        count_along = keep.tile([P, QUAD], F32, name="count_along", tag="staged1", align_bytes=64)
+        nc.vector.tensor_tensor_scan(count_along[:], ones[:], ones[:], 0.0, ALU.mult, ALU.add)
         ident = keep.tile([P, P], F32, name="ident")
-        make_identity(nc, ident[:])
-        noise_sb = keep.tile([P, BLOCKS, 1], F32, name="noise_sb")
-        with nc.allow_non_contiguous_dma(reason="one noise value a partition and block"):
-            nc.scalar.dma_start(noise_sb[:], noise.rearrange("(b p) o -> p b o", p=P))
+        nc.vector.memset(ident[:], 0.0)
+        count_down = keep.tile([P, QUAD], F32, name="count_down", tag="small", align_bytes=64)
+        nc.vector.transpose(count_down[:], count_along[:])
+        for q in range(P // QUAD):
+            quad = slice(q * QUAD, (q + 1) * QUAD)
+            nc.vector.tensor_tensor(ident[quad, quad], count_along[quad, :], count_down[quad, :], ALU.is_equal)
         power = [keep.tile([P, S + SPARE], F32, name="power%d" % b) for b in range(BLOCKS)]
         weighted = [keep.tile([P, S + SPARE], F32, name="weighted%d" % b) for b in range(BLOCKS)]
         for window in power + weighted:
-            nc.vector.memset(window[:, S:], 0.0)
+            nc.scalar.activation(window[:, S:], ident[:, :SPARE], ACT.Sigmoid)
 
         offs_sb = lists.tile([P, S // 16], U16, name="offs_sb")
         pos_sb = [lists.tile([P, S // 16], U16, name="pos_sb%d" % d) for d in range(D)]
         nc.sync.dma_start(offs_sb[:], offs)
-        nc.sync.dma_start(pos_sb[0][:], pos1)
         for q in range(4):
-            nc.scalar.dma_start(
+            (nc.sync, nc.scalar)[q % 2].dma_start(
                 xs_all[32 * q : 32 * q + 4, :].bitcast(I32), x_scales[0, 4 * q : 4 * q + 4, :].bitcast(I32)
             )
         w_rows = w1.rearrange("(p t) n -> p t n", t=PACK)
-        w_raw = [keep.tile([P, PACK, P], F32, name="w_raw%d" % b, tag="staged%d" % b) for b in range(BLOCKS)]
-        xw_all = keep.tile([P, T], U32, name="xw_all")
+        w_raw = [keep.tile([P, PACK, P], F32, name="w_raw%d" % b, tag="staged%d" % b, align_bytes=64) for b in range(BLOCKS)]
+        xw_all = keep.tile([P, T], U32, name="xw_all", tag="words", align_bytes=64)
         nc.sync.dma_start(w_raw[0][:], w_rows[:, :, 0:P])
         nc.sync.dma_start(xw_all[:].bitcast(I32), x_words[0].rearrange("p n t -> p (n t)").bitcast(I32))
         nc.sync.dma_start(w_raw[1][:], w_rows[:, :, P : 2 * P])
+        small = keep.tile([P, P + BLOCKS], F32, name="small", tag="small", align_bytes=64)
+        nc.sync.dma_start(small[0:64, :P], hh[0:16, :].rearrange("r (t c) -> (r t) c", c=P))
+        nc.sync.dma_start(small[64:128, :P], pri[0:16, :].rearrange("r (t c) -> (r t) c", c=P))
+        with nc.allow_non_contiguous_dma(reason="one noise value a partition and block"):
+            nc.sync.dma_start(small[:, P:].unsqueeze(2), noise.rearrange("(b p) o -> p b o", p=P))
+        nc.sync.dma_start(pos_sb[0][:], pos1)
         nc.sync.dma_start(pos_sb[1][:], pos2)
         nc.sync.dma_start(pos_sb[2][:], pos3)
 
         w_codes = []
         w_scales = []
 
-        def quantise(b):
+        def quantise(b, cast):
             grouped = keep.tile([P, P, PACK], BF16, name="grouped%d" % b, tag="grouped%d" % b, align_bytes=64)
-            nc.vector.tensor_copy(
+            cast(
                 grouped[:].rearrange("p (c i) t -> p c t i", i=4),
                 w_raw[b][:].rearrange("p t (c i) -> p c t i", i=4),
             )
-            w_codes.append(keep.tile([P, P], U32, name="w_codes%d" % b, align_bytes=64))
+            w_codes.append(keep.tile([P, P], U32, name="w_codes%d" % b, tag=("codes0", "words")[b], align_bytes=64))
             w_scales.append(keep.tile([P, P], U8, name="w_scales%d" % b, align_bytes=64))
             nc.vector.quantize_mx(
                 out=w_codes[b][:].bitcast(FP8X4),
@@ -86,8 +94,8 @@ def tile_picked_ywmmse_tx_p_kernel(tc, x_words, x_scales, w1, gain, hh, noise, p
                 in_=grouped[:].rearrange("p c t -> p (c t)"),
             )
 
-        quantise(0)
-        gain_first = keep.tile([P, S], F32, name="gain_first", tag="staged0")
+        quantise(0, nc.vector.tensor_copy)
+        gain_first = keep.tile([P, S], F32, name="gain_first", tag="staged0", align_bytes=64)
         gain_rest = keep.tile([P, D - 1, S], F32, name="gain_rest", tag="grouped0", align_bytes=64)
         nc.sync.dma_start(gain_first[:], gain[0])
         nc.sync.dma_start(gain_rest[:], gain[1:D].rearrange("d p s -> p d s"))
@@ -96,23 +104,6 @@ def tile_picked_ywmmse_tx_p_kernel(tc, x_words, x_scales, w1, gain, hh, noise, p
         xs = keep.tile([P, S], U8, name="xs", align_bytes=64)
         xw = keep.tile([P, S], U32, name="xw", align_bytes=64)
         nc.vector.tensor_copy(xs[:], xs_all[:].indirect(offs_sb[:]))
-
-        turned = bank(5, "turned", 1)
-        nc.tensor.transpose(turned[:, 0, :], rows[:], ident[:])
-        h_abs = keep.tile([P, TILES], F32, name="h_abs")
-        nc.scalar.activation(h_abs[:], turned[:, 0, 0:TILES], ACT.Abs)
-        pri_col = keep.tile([P, TILES], F32, name="pri_col")
-        nc.scalar.copy(pri_col[:], turned[:, 0, 64 : 64 + TILES])
-        pri_h = keep.tile([P, TILES], F32, name="pri_h")
-        nc.vector.scalar_tensor_tensor(pri_h[:], h_abs[:], 1e-10, pri_col[:], ALU.max, ALU.mult)
-        pri_pos = keep.tile([P, TILES], F32, name="pri_pos")
-        nc.vector.tensor_scalar(pri_pos[:], pri_col[:], 1e-30, None, ALU.max)
-        pri_hh = keep.tile([P, TILES], F32, name="pri_hh")
-        nc.vector.tensor_tensor(pri_hh[:], pri_h[:], h_abs[:], ALU.mult)
-        inv_pri = keep.tile([P, TILES], F32, name="inv_pri")
-        nc.vector.reciprocal(inv_pri[:], pri_pos[:])
-        pri_hh_sq = keep.tile([P, TILES], F32, name="pri_hh_sq")
-        nc.scalar.activation(pri_hh_sq[:], pri_hh[:], ACT.Square)
 
         def add_turned(into, term, first, last):
             for place, (target, slot, t) in enumerate(into):
@@ -126,10 +117,11 @@ def tile_picked_ywmmse_tx_p_kernel(tc, x_words, x_scales, w1, gain, hh, noise, p
         def whole(target):
             return [(target, t, t) for t in range(TILES)]
 
-        heard = [bank(b, "heard%d" % b) for b in range(BLOCKS)]
+        def halves(banks):
+            return [(banks[t // 2], t % 2, t) for t in range(TILES)]
 
         def add_noise(b):
-            add_turned(whole(heard[b]), lambda t: noise_sb[:, b, :].to_broadcast([P, P]), False, False)
+            add_turned(halves(heard[b]), lambda t: small[:, P + b : P + b + 1].to_broadcast([P, P]), False, False)
 
         def product(b, index, lo, hi):
             y = bank(index, "y", (hi - lo) // P)
@@ -143,24 +135,39 @@ def tile_picked_ywmmse_tx_p_kernel(tc, x_words, x_scales, w1, gain, hh, noise, p
             lo, hi = half * HALF, (half + 1) * HALF
             nc.vector.tensor_copy(xw[:, lo:hi], xw_all[:].indirect(offs_sb[:, lo // 16 : hi // 16]))
             product(0, 2 + half, lo, hi)
-        quantise(1)
+        quantise(1, nc.scalar.copy)
         product(1, 4, 0, S)
-        hh_sb = keep.tile([P, S], F32, name="hh_sb", tag="staged1")
-        nc.sync.dma_start(hh_sb[:], hh)
+
+        turned = bank(5, "turned", 1)
+        nc.tensor.transpose(turned[:, 0, :], small[:, :P], ident[:])
+        cols = keep.tile([P, 2, TILES], F32, name="cols", tag="grouped1", align_bytes=64)
+        nc.vector.tensor_copy(cols[:], turned[:, 0, :].rearrange("p (a r) -> p a r", a=2)[:, :, 0:TILES])
+        h_sq = keep.tile([P, TILES], F32, name="h_sq")
+        nc.vector.tensor_tensor(h_sq[:], cols[:, 0, :], cols[:, 0, :], ALU.mult)
+        pri_pos = keep.tile([P, TILES], F32, name="pri_pos")
+        nc.vector.tensor_scalar(pri_pos[:], cols[:, 1, :], 1e-30, None, ALU.max)
+        pri_hh = keep.tile([P, TILES], F32, name="pri_hh")
+        nc.vector.tensor_tensor(pri_hh[:], h_sq[:], cols[:, 1, :], ALU.mult)
+        inv_pri = keep.tile([P, TILES], F32, name="inv_pri")
+        nc.vector.reciprocal(inv_pri[:], pri_pos[:])
+        own = bank(7, "own")
+        for t in range(TILES):
+            nc.tensor.transpose(own[:, t, :], h_sq[:, t : t + 1].to_broadcast([P, P]), ident[:])
 
         inv_amp = []
         for b in range(BLOCKS):
-            power_t = bank(5 + b, "power_t")
+            power_t = bank(4 + b, "power_t")
             for t in range(TILES):
                 nc.tensor.transpose(power_t[:, t, :], power[b][:, t * P : (t + 1) * P], ident[:])
-            inv_amp.append(keep.tile([P, TILES, P], F32, name="inv_amp%d" % b, tag="inv_amp%d" % b))
+            inv_amp.append([
+                keep.tile([P, 2, P], F32, name="inv_amp%d%d" % (b, h), tag="inv_amp%d%d" % (b, h)) for h in range(2)
+            ])
             for t in range(TILES):
                 nc.scalar.activation(
-                    inv_amp[b][:, t, :], power_t[:, t, :], ACT.Abs_reciprocal_sqrt,
-                    bias=1e-30, scale=pri_hh_sq[:, t : t + 1],
+                    inv_amp[b][t // 2][:, t % 2, :], power_t[:, t, :], ACT.Abs_reciprocal_sqrt,
+                    bias=1e-30, scale=pri_hh[:, t : t + 1],
                 )
-        own = keep.tile([P, S], F32, name="own")
-        nc.scalar.activation(own[:], hh_sb[:], ACT.Square)
+        heard = [[bank(2 * b + h, "heard", 2) for h in range(2)] for b in range(BLOCKS)]
 
         def neighbour(into, window, d, tag=None, first=False):
             lo, hi = into[0][2] * P, (into[-1][2] + 1) * P
@@ -174,26 +181,33 @@ def tile_picked_ywmmse_tx_p_kernel(tc, x_words, x_scales, w1, gain, hh, noise, p
             add_turned(into, lambda t: term[:, t * P - lo : (t + 1) * P - lo], first, d == D - 1)
 
         scaled = [keep.tile([P, TILES, P], F32, name="scaled%d" % b, tag="scaled%d" % b) for b in range(BLOCKS)]
-        squared = [keep.tile([P, TILES, P], F32, name="squared%d" % b, tag="squared%d" % b) for b in range(BLOCKS)]
 
-        def scale_heard(b):
-            nc.vector.tensor_tensor(scaled[b][:], heard[b][:], inv_amp[b][:], ALU.mult)
-            for t in range(TILES):
-                nc.scalar.activation(squared[b][:, t, :], scaled[b][:, t, :], ACT.Square, scale=pri_h[:, t : t + 1])
+        root = [keep.tile([P, S], F32, name="root%d" % b) for b in range(BLOCKS)]
 
-        def weigh(b):
-            total = keep.tile([P, TILES, P], F32, name="total%d" % b)
-            nc.vector.tensor_tensor(total[:], squared[b][:], heard[b][:], ALU.add)
-            root = keep.tile([P, TILES, P], F32, name="root%d" % b)
-            back = bank(2 + b, "back")
-            for t in range(TILES):
-                nc.scalar.activation(root[:, t, :], total[:, t, :], ACT.Abs_reciprocal_sqrt, scale=inv_pri[:, t : t + 1])
-                nc.tensor.transpose(back[:, t, :], root[:, t, :], ident[:])
-            nc.scalar.activation(weighted[b][:, :S], flat(back), ACT.Square)
+        def weigh_half(b, h):
+            pair = slice(2 * h, 2 * h + 2)
+            nc.vector.tensor_tensor(scaled[b][:, pair, :], heard[b][h][:], inv_amp[b][h][:], ALU.mult)
+            linear = ring.tile([P, 2, P], F32, name="linear")
+            for i in range(2):
+                nc.scalar.activation(
+                    linear[:, i, :], heard[b][h][:, i, :], ACT.Copy, scale=inv_pri[:, 2 * h + i : 2 * h + i + 1]
+                )
+            squared = ring.tile([P, 2, P], F32, name="squared")
+            nc.scalar.activation(squared[:], scaled[b][:, pair, :], ACT.Square)
+            back = bank(4 + h, "back", 2)
+            into = [(back, i, i) for i in range(2)]
+            add_turned(into, lambda i: linear[:, i, :], True, False)
+            add_turned(into, lambda i: squared[:, i, :], False, True)
+            return back
 
-        def own_term(b, into):
-            term = ring.tile([P, S], F32, name="term")
-            nc.vector.tensor_tensor(term[:], weighted[b][:, :S], own[:], ALU.mult)
+        def weigh(b, back):
+            for h in range(2):
+                nc.scalar.activation(root[b][:, h * HALF : (h + 1) * HALF], flat(back[h]), ACT.Abs_reciprocal_sqrt)
+            nc.scalar.activation(weighted[b][:, :S], root[b][:], ACT.Square)
+
+        def own_term(b, into, tag):
+            term = keep.tile([P, S], F32, name="own_term", tag=tag)
+            nc.vector.tensor_tensor(term[:], weighted[b][:, :S], flat(own), ALU.mult)
             add_turned(into, lambda t: term[:, t * P : (t + 1) * P], True, False)
 
         def finish(b, sums, first, count, index):
@@ -201,39 +215,53 @@ def tile_picked_ywmmse_tx_p_kernel(tc, x_words, x_scales, w1, gain, hh, noise, p
             nc.vector.scalar_tensor_tensor(
                 denom[:], sums[:], 0.3, scaled[b][:, first : first + count, :], ALU.add, ALU.mult
             )
-            root = keep.tile([P, count, P], F32, name="root_out%d" % index)
-            nc.scalar.activation(root[:], denom[:], ACT.Abs_reciprocal_sqrt)
+            out_root = keep.tile([P, count, P], F32, name="out_root%d" % index)
             back = bank(index, "back_out", count)
             for t in range(count):
-                nc.tensor.transpose(back[:, t, :], root[:, t, :], ident[:])
+                nc.scalar.activation(
+                    out_root[:, t, :], denom[:, t, :], ACT.Abs_reciprocal_sqrt,
+                    scale=inv_root[:, first + t : first + t + 1],
+                )
+                nc.tensor.transpose(back[:, t, :], out_root[:, t, :], ident[:])
             result = keep.tile([P, count * P], F32, name="result%d" % index)
             nc.scalar.activation(result[:], flat(back), ACT.Square)
             nc.sync.dma_start(out[b * P : (b + 1) * P, first * P : (first + count) * P], result[:])
 
-        neighbour(whole(heard[0]), power[0], 0, first=True)
+        first_block, second_block = halves(heard[0]), halves(heard[1])
+        neighbour(first_block, power[0], 0, first=True)
         add_noise(0)
-        for d in range(1, D):
-            neighbour(whole(heard[0]), power[0], d)
-        neighbour(whole(heard[1]), power[1], 0, first=True)
+        neighbour(first_block, power[0], 1)
+        neighbour(first_block[:2], power[0], 2)
+        neighbour(first_block[2:], power[0], 2)
+        back = []
+        for h in range(2):
+            back.append(weigh_half(0, h))
+            neighbour(second_block[2 * h : 2 * h + 2], power[1], 0, "inv_amp0%d" % h, first=True)
         add_noise(1)
-        scale_heard(0)
-        neighbour(whole(heard[1]), power[1], 1, "inv_amp0")
-        weigh(0)
-        neighbour(whole(heard[1]), power[1], 2, "squared0")
-        scale_heard(1)
-        sums = bank(4, "sums")
-        own_term(0, whole(sums))
-        neighbour(whole(sums), weighted[0], 0)
-        weigh(1)
-        neighbour(whole(sums), weighted[0], 1, "squared1")
+        inv_root = keep.tile([P, TILES], F32, name="inv_root", tag="small", align_bytes=64)
+        nc.scalar.activation(inv_root[:], pri_hh[:], ACT.Abs_reciprocal_sqrt, bias=1e-30)
+        weigh(0, back)
+        neighbour(second_block, power[1], 1)
+        neighbour(second_block[:2], power[1], 2)
+        neighbour(second_block[2:], power[1], 2)
+        sums = bank(6, "sums")
+        back = [weigh_half(1, 0)]
+        own_term(0, whole(sums), "inv_amp10")
+        back.append(weigh_half(1, 1))
+        weigh(1, back)
+        neighbour(whole(sums), weighted[0], 0, "inv_amp11")
+        neighbour(whole(sums), weighted[0], 1)
         neighbour(whole(sums), weighted[0], 2)
-        halves = [bank(h, "sums_half", 2) for h in range(2)]
-        split = [(halves[t // 2], t % 2, t) for t in range(TILES)]
-        own_term(1, split)
+        parts = [bank(0, "sums_a", 2), bank(1, "sums_b", 1), bank(2, "sums_c", 1)]
+        split = [(parts[0], 0, 0), (parts[0], 1, 1), (parts[1], 0, 2), (parts[2], 0, 3)]
+        own_term(1, split, "own_term1")
         neighbour(split, weighted[1], 0)
-        finish(0, sums, 0, TILES, 2)
-        neighbour(split, weighted[1], 1, "scaled0")
+        finish(0, sums, 0, TILES, 4)
+        neighbour(split[:2], weighted[1], 1, "scaled0")
         neighbour(split[:2], weighted[1], 2)
-        neighbour(split[2:], weighted[1], 2)
-        finish(1, halves[0], 0, 2, 3)
-        finish(1, halves[1], 2, 2, 5)
+        neighbour(split[2:], weighted[1], 1)
+        finish(1, parts[0], 0, 2, 5)
+        neighbour(split[2:3], weighted[1], 2)
+        neighbour(split[3:], weighted[1], 2)
+        finish(1, parts[1], 2, 1, 3)
+        finish(1, parts[2], 3, 1, 6)

@@ -39,7 +39,7 @@ def tile_picked_ywmmse_tx_p_kernel(tc, x_words, x_scales, w1, gain, hh, noise, p
 
         xs_all = keep.tile([P, T], U8, name="xs_all")
         nc.gpsimd.memset(xs_all[:].bitcast(I32), 0)
-        ones = keep.tile([P, QUAD], F32, name="ones", tag="words", align_bytes=64)
+        ones = keep.tile([P, QUAD], F32, name="ones", tag="inv_amp01", align_bytes=64)
         nc.gpsimd.memset(ones[:], 1.0)
         count_along = keep.tile([P, QUAD], F32, name="count_along", tag="staged1", align_bytes=64)
         nc.vector.tensor_tensor_scan(count_along[:], ones[:], ones[:], 0.0, ALU.mult, ALU.add)
@@ -58,21 +58,22 @@ def tile_picked_ywmmse_tx_p_kernel(tc, x_words, x_scales, w1, gain, hh, noise, p
         offs_sb = lists.tile([P, S // 16], U16, name="offs_sb")
         pos_sb = [lists.tile([P, S // 16], U16, name="pos_sb%d" % d) for d in range(D)]
         nc.sync.dma_start(offs_sb[:], offs)
+        noise_sb = keep.tile([P, BLOCKS, 1], F32, name="noise_sb")
+        with nc.allow_non_contiguous_dma(reason="one noise value a partition and block"):
+            nc.scalar.dma_start(noise_sb[:], noise.rearrange("(b p) o -> p b o", p=P))
         for q in range(4):
             (nc.sync, nc.scalar)[q % 2].dma_start(
                 xs_all[32 * q : 32 * q + 4, :].bitcast(I32), x_scales[0, 4 * q : 4 * q + 4, :].bitcast(I32)
             )
         w_rows = w1.rearrange("(p t) n -> p t n", t=PACK)
         w_raw = [keep.tile([P, PACK, P], F32, name="w_raw%d" % b, tag="staged%d" % b, align_bytes=64) for b in range(BLOCKS)]
-        xw_all = keep.tile([P, T], U32, name="xw_all", tag="words", align_bytes=64)
+        xw_all = keep.tile([P, T], U32, name="xw_all", tag="inv_amp01", align_bytes=64)
         nc.sync.dma_start(w_raw[0][:], w_rows[:, :, 0:P])
         nc.sync.dma_start(xw_all[:].bitcast(I32), x_words[0].rearrange("p n t -> p (n t)").bitcast(I32))
         nc.sync.dma_start(w_raw[1][:], w_rows[:, :, P : 2 * P])
-        small = keep.tile([P, P + BLOCKS], F32, name="small", tag="small", align_bytes=64)
+        small = keep.tile([P, P], F32, name="small", tag="small", align_bytes=64)
         nc.sync.dma_start(small[0:64, :P], hh[0:16, :].rearrange("r (t c) -> (r t) c", c=P))
         nc.sync.dma_start(small[64:128, :P], pri[0:16, :].rearrange("r (t c) -> (r t) c", c=P))
-        with nc.allow_non_contiguous_dma(reason="one noise value a partition and block"):
-            nc.sync.dma_start(small[:, P:].unsqueeze(2), noise.rearrange("(b p) o -> p b o", p=P))
         nc.sync.dma_start(pos_sb[0][:], pos1)
         nc.sync.dma_start(pos_sb[1][:], pos2)
         nc.sync.dma_start(pos_sb[2][:], pos3)
@@ -86,8 +87,8 @@ def tile_picked_ywmmse_tx_p_kernel(tc, x_words, x_scales, w1, gain, hh, noise, p
                 grouped[:].rearrange("p (c i) t -> p c t i", i=4),
                 w_raw[b][:].rearrange("p t (c i) -> p c t i", i=4),
             )
-            w_codes.append(keep.tile([P, P], U32, name="w_codes%d" % b, tag=("codes0", "words")[b], align_bytes=64))
-            w_scales.append(keep.tile([P, P], U8, name="w_scales%d" % b, align_bytes=64))
+            w_codes.append(keep.tile([P, P], U32, name="w_codes%d" % b, tag=("codes0", "inv_amp01")[b], align_bytes=64))
+            w_scales.append(keep.tile([P, P], U8, name="w_scales%d" % b, tag=("scales0", "inv_amp00")[b], align_bytes=64))
             nc.vector.quantize_mx(
                 out=w_codes[b][:].bitcast(FP8X4),
                 scales=w_scales[b][:],
@@ -120,8 +121,9 @@ def tile_picked_ywmmse_tx_p_kernel(tc, x_words, x_scales, w1, gain, hh, noise, p
         def halves(banks):
             return [(banks[t // 2], t % 2, t) for t in range(TILES)]
 
-        def add_noise(b):
-            add_turned(halves(heard[b]), lambda t: small[:, P + b : P + b + 1].to_broadcast([P, P]), False, False)
+        heard = [[bank(2 * b + h, "heard", 2) for h in range(2)] for b in range(BLOCKS)]
+        for b in range(BLOCKS):
+            add_turned(halves(heard[b]), lambda t: noise_sb[:, b, :].to_broadcast([P, P]), True, False)
 
         def product(b, index, lo, hi):
             y = bank(index, "y", (hi - lo) // P)
@@ -134,7 +136,7 @@ def tile_picked_ywmmse_tx_p_kernel(tc, x_words, x_scales, w1, gain, hh, noise, p
         for half in range(2):
             lo, hi = half * HALF, (half + 1) * HALF
             nc.vector.tensor_copy(xw[:, lo:hi], xw_all[:].indirect(offs_sb[:, lo // 16 : hi // 16]))
-            product(0, 2 + half, lo, hi)
+            product(0, 6 + half, lo, hi)
         quantise(1, nc.scalar.copy)
         product(1, 4, 0, S)
 
@@ -156,57 +158,56 @@ def tile_picked_ywmmse_tx_p_kernel(tc, x_words, x_scales, w1, gain, hh, noise, p
 
         inv_amp = []
         for b in range(BLOCKS):
-            power_t = bank(4 + b, "power_t")
+            power_t = bank((6, 4)[b], "power_t")
             for t in range(TILES):
                 nc.tensor.transpose(power_t[:, t, :], power[b][:, t * P : (t + 1) * P], ident[:])
             inv_amp.append([
-                keep.tile([P, 2, P], F32, name="inv_amp%d%d" % (b, h), tag="inv_amp%d%d" % (b, h)) for h in range(2)
+                keep.tile([P, 2, P], F32, name="inv_amp%d%d" % (b, h), tag="inv_amp%d%d" % (b, h), align_bytes=64) for h in range(2)
             ])
             for t in range(TILES):
                 nc.scalar.activation(
                     inv_amp[b][t // 2][:, t % 2, :], power_t[:, t, :], ACT.Abs_reciprocal_sqrt,
                     bias=1e-30, scale=pri_hh[:, t : t + 1],
                 )
-        heard = [[bank(2 * b + h, "heard", 2) for h in range(2)] for b in range(BLOCKS)]
 
-        def neighbour(into, window, d, tag=None, first=False):
+        def neighbour(into, window, d, tag=None):
             lo, hi = into[0][2] * P, (into[-1][2] + 1) * P
             if tag is None:
                 term = ring.tile([P, hi - lo], F32, name="term")
             else:
-                term = keep.tile([P, hi - lo], F32, name="term", tag=tag)
+                term = keep.tile([P, hi - lo], F32, name="term", tag=tag, align_bytes=64)
             nc.vector.tensor_tensor(
                 term[:], window[:].indirect(pos_sb[d][:, lo // 16 : hi // 16]), gain_sb[d][:, lo:hi], ALU.mult
             )
-            add_turned(into, lambda t: term[:, t * P - lo : (t + 1) * P - lo], first, d == D - 1)
+            add_turned(into, lambda t: term[:, t * P - lo : (t + 1) * P - lo], False, d == D - 1)
 
-        scaled = [keep.tile([P, TILES, P], F32, name="scaled%d" % b, tag="scaled%d" % b) for b in range(BLOCKS)]
+        scaled = [keep.tile([P, TILES, P], F32, name="scaled0", tag="scaled0", align_bytes=64)]
 
-        root = [keep.tile([P, S], F32, name="root%d" % b) for b in range(BLOCKS)]
 
         def weigh_half(b, h):
             pair = slice(2 * h, 2 * h + 2)
             nc.vector.tensor_tensor(scaled[b][:, pair, :], heard[b][h][:], inv_amp[b][h][:], ALU.mult)
-            linear = ring.tile([P, 2, P], F32, name="linear")
+            linear = keep.tile([P, 2, P], F32, name="linear", tag="linear%d%d" % (b, h), align_bytes=64)
             for i in range(2):
                 nc.scalar.activation(
                     linear[:, i, :], heard[b][h][:, i, :], ACT.Copy, scale=inv_pri[:, 2 * h + i : 2 * h + i + 1]
                 )
-            squared = ring.tile([P, 2, P], F32, name="squared")
+            squared = keep.tile([P, 2, P], F32, name="squared", tag="squared%d%d" % (b, h), align_bytes=64)
             nc.scalar.activation(squared[:], scaled[b][:, pair, :], ACT.Square)
-            back = bank(4 + h, "back", 2)
+            back = bank(5 + h, "back", 2)
             into = [(back, i, i) for i in range(2)]
             add_turned(into, lambda i: linear[:, i, :], True, False)
             add_turned(into, lambda i: squared[:, i, :], False, True)
             return back
 
         def weigh(b, back):
+            root = keep.tile([P, S], F32, name="root", tag="root%d" % b, align_bytes=64)
             for h in range(2):
-                nc.scalar.activation(root[b][:, h * HALF : (h + 1) * HALF], flat(back[h]), ACT.Abs_reciprocal_sqrt)
-            nc.scalar.activation(weighted[b][:, :S], root[b][:], ACT.Square)
+                nc.scalar.activation(root[:, h * HALF : (h + 1) * HALF], flat(back[h]), ACT.Abs_reciprocal_sqrt)
+            nc.scalar.activation(weighted[b][:, :S], root[:], ACT.Square)
 
         def own_term(b, into, tag):
-            term = keep.tile([P, S], F32, name="own_term", tag=tag)
+            term = keep.tile([P, S], F32, name="own_term", tag=tag, align_bytes=64)
             nc.vector.tensor_tensor(term[:], weighted[b][:, :S], flat(own), ALU.mult)
             add_turned(into, lambda t: term[:, t * P : (t + 1) * P], True, False)
 
@@ -215,7 +216,7 @@ def tile_picked_ywmmse_tx_p_kernel(tc, x_words, x_scales, w1, gain, hh, noise, p
             nc.vector.scalar_tensor_tensor(
                 denom[:], sums[:], 0.3, scaled[b][:, first : first + count, :], ALU.add, ALU.mult
             )
-            out_root = keep.tile([P, count, P], F32, name="out_root%d" % index)
+            out_root = keep.tile([P, count, P], F32, name="out_root", tag="out_root%d" % index, align_bytes=64)
             back = bank(index, "back_out", count)
             for t in range(count):
                 nc.scalar.activation(
@@ -228,40 +229,40 @@ def tile_picked_ywmmse_tx_p_kernel(tc, x_words, x_scales, w1, gain, hh, noise, p
             nc.sync.dma_start(out[b * P : (b + 1) * P, first * P : (first + count) * P], result[:])
 
         first_block, second_block = halves(heard[0]), halves(heard[1])
-        neighbour(first_block, power[0], 0, first=True)
-        add_noise(0)
+        neighbour(first_block, power[0], 0)
         neighbour(first_block, power[0], 1)
         neighbour(first_block[:2], power[0], 2)
         neighbour(first_block[2:], power[0], 2)
         back = []
         for h in range(2):
             back.append(weigh_half(0, h))
-            neighbour(second_block[2 * h : 2 * h + 2], power[1], 0, "inv_amp0%d" % h, first=True)
-        add_noise(1)
-        inv_root = keep.tile([P, TILES], F32, name="inv_root", tag="small", align_bytes=64)
+            neighbour(second_block[2 * h : 2 * h + 2], power[1], 0, "inv_amp0%d" % h)
+        inv_root = keep.tile([P, TILES], F32, name="inv_root", tag="linear00", align_bytes=64)
         nc.scalar.activation(inv_root[:], pri_hh[:], ACT.Abs_reciprocal_sqrt, bias=1e-30)
         weigh(0, back)
-        neighbour(second_block, power[1], 1)
+        neighbour(second_block[:2], power[1], 1, "squared00")
+        neighbour(second_block[2:], power[1], 1, "squared01")
         neighbour(second_block[:2], power[1], 2)
         neighbour(second_block[2:], power[1], 2)
-        sums = bank(6, "sums")
+        sums = bank(4, "sums")
+        scaled.append(keep.tile([P, TILES, P], F32, name="scaled1", tag="root0", align_bytes=64))
         back = [weigh_half(1, 0)]
         own_term(0, whole(sums), "inv_amp10")
         back.append(weigh_half(1, 1))
         weigh(1, back)
         neighbour(whole(sums), weighted[0], 0, "inv_amp11")
-        neighbour(whole(sums), weighted[0], 1)
+        neighbour(whole(sums), weighted[0], 1, "squared11")
         neighbour(whole(sums), weighted[0], 2)
         parts = [bank(0, "sums_a", 2), bank(1, "sums_b", 1), bank(2, "sums_c", 1)]
         split = [(parts[0], 0, 0), (parts[0], 1, 1), (parts[1], 0, 2), (parts[2], 0, 3)]
         own_term(1, split, "own_term1")
-        neighbour(split, weighted[1], 0)
-        finish(0, sums, 0, TILES, 4)
-        neighbour(split[:2], weighted[1], 1, "scaled0")
-        neighbour(split[:2], weighted[1], 2)
+        finish(0, sums, 0, TILES, 5)
+        neighbour(split, weighted[1], 0, "scaled0")
+        neighbour(split[:2], weighted[1], 1)
+        neighbour(split[:2], weighted[1], 2, "out_root5")
         neighbour(split[2:], weighted[1], 1)
-        finish(1, parts[0], 0, 2, 5)
+        finish(1, parts[0], 0, 2, 6)
         neighbour(split[2:3], weighted[1], 2)
         neighbour(split[3:], weighted[1], 2)
         finish(1, parts[1], 2, 1, 3)
-        finish(1, parts[2], 3, 1, 6)
+        finish(1, parts[2], 3, 1, 4)

@@ -75,8 +75,6 @@ def tile_picked_ywmmse_tx_p_kernel(tc, x_words, x_scales, w1, gain, hh, noise, p
         nc.sync.dma_start(small[0:64, :P], hh[0:16, :].rearrange("r (t c) -> (r t) c", c=P))
         nc.sync.dma_start(small[64:128, :P], pri[0:16, :].rearrange("r (t c) -> (r t) c", c=P))
         nc.sync.dma_start(pos_sb[0][:], pos1)
-        nc.sync.dma_start(pos_sb[1][:], pos2)
-        nc.sync.dma_start(pos_sb[2][:], pos3)
 
         w_codes = []
         w_scales = []
@@ -100,6 +98,8 @@ def tile_picked_ywmmse_tx_p_kernel(tc, x_words, x_scales, w1, gain, hh, noise, p
         gain_rest = keep.tile([P, D - 1, S], F32, name="gain_rest", tag="grouped0", align_bytes=64)
         nc.sync.dma_start(gain_first[:], gain[0])
         nc.sync.dma_start(gain_rest[:], gain[1:D].rearrange("d p s -> p d s"))
+        nc.sync.dma_start(pos_sb[1][:], pos2)
+        nc.sync.dma_start(pos_sb[2][:], pos3)
         gain_sb = [gain_first[:]] + [gain_rest[:, d, :] for d in range(D - 1)]
 
         xs = keep.tile([P, S], U8, name="xs", align_bytes=64)
@@ -184,16 +184,14 @@ def tile_picked_ywmmse_tx_p_kernel(tc, x_words, x_scales, w1, gain, hh, noise, p
         scaled = [keep.tile([P, TILES, P], F32, name="scaled0", tag="scaled0", align_bytes=64)]
 
 
-        def weigh_half(b, h):
+        def weigh_half(b, h, linear, squared):
             pair = slice(2 * h, 2 * h + 2)
             nc.vector.tensor_tensor(scaled[b][:, pair, :], heard[b][h][:], inv_amp[b][h][:], ALU.mult)
-            linear = keep.tile([P, 2, P], F32, name="linear", tag="linear%d%d" % (b, h), align_bytes=64)
             for i in range(2):
                 nc.scalar.activation(
                     linear[:, i, :], heard[b][h][:, i, :], ACT.Copy, scale=inv_pri[:, 2 * h + i : 2 * h + i + 1]
                 )
-            squared = keep.tile([P, 2, P], F32, name="squared", tag="squared%d%d" % (b, h), align_bytes=64)
-            nc.scalar.activation(squared[:], scaled[b][:, pair, :], ACT.Square)
+            nc.scalar.activation(squared, scaled[b][:, pair, :], ACT.Square)
             back = bank(5 + h, "back", 2)
             into = [(back, i, i) for i in range(2)]
             add_turned(into, lambda i: linear[:, i, :], True, False)
@@ -201,10 +199,11 @@ def tile_picked_ywmmse_tx_p_kernel(tc, x_words, x_scales, w1, gain, hh, noise, p
             return back
 
         def weigh(b, back):
-            root = keep.tile([P, S], F32, name="root", tag="root%d" % b, align_bytes=64)
+            root = [keep.tile([P, HALF], F32, name="root", tag="root%d%d" % (b, h), align_bytes=64) for h in range(2)]
             for h in range(2):
-                nc.scalar.activation(root[:, h * HALF : (h + 1) * HALF], flat(back[h]), ACT.Abs_reciprocal_sqrt)
-            nc.scalar.activation(weighted[b][:, :S], root[:], ACT.Square)
+                nc.scalar.activation(root[h][:], flat(back[h]), ACT.Abs_reciprocal_sqrt)
+            for h in range(2):
+                nc.scalar.activation(weighted[b][:, h * HALF : (h + 1) * HALF], root[h][:], ACT.Square)
 
         def own_term(b, into, tag):
             term = keep.tile([P, S], F32, name="own_term", tag=tag, align_bytes=64)
@@ -235,31 +234,33 @@ def tile_picked_ywmmse_tx_p_kernel(tc, x_words, x_scales, w1, gain, hh, noise, p
         neighbour(first_block[2:], power[0], 2)
         back = []
         for h in range(2):
-            back.append(weigh_half(0, h))
+            linear = keep.tile([P, 2, P], F32, name="linear", tag="linear%d" % h, align_bytes=64)
+            squared = keep.tile([P, 2, P], F32, name="squared", tag="squared%d" % h, align_bytes=64)
+            back.append(weigh_half(0, h, linear[:], squared[:]))
             neighbour(second_block[2 * h : 2 * h + 2], power[1], 0, "inv_amp0%d" % h)
-        inv_root = keep.tile([P, TILES], F32, name="inv_root", tag="linear00", align_bytes=64)
+        inv_root = keep.tile([P, TILES], F32, name="inv_root", tag="linear0", align_bytes=64)
         nc.scalar.activation(inv_root[:], pri_hh[:], ACT.Abs_reciprocal_sqrt, bias=1e-30)
         weigh(0, back)
-        neighbour(second_block[:2], power[1], 1, "squared00")
-        neighbour(second_block[2:], power[1], 1, "squared01")
-        neighbour(second_block[:2], power[1], 2)
+        neighbour(second_block, power[1], 1, "squared0")
+        neighbour(second_block[:2], power[1], 2, "squared1")
         neighbour(second_block[2:], power[1], 2)
         sums = bank(4, "sums")
-        scaled.append(keep.tile([P, TILES, P], F32, name="scaled1", tag="root0", align_bytes=64))
-        back = [weigh_half(1, 0)]
-        own_term(0, whole(sums), "inv_amp10")
-        back.append(weigh_half(1, 1))
+        scaled.append(keep.tile([P, TILES, P], F32, name="scaled1", tag="scaled1", align_bytes=64))
+        linear = keep.tile([P, TILES, P], F32, name="linear", tag="root01", align_bytes=64)
+        squared = keep.tile([P, TILES, P], F32, name="squared", tag="root00", align_bytes=64)
+        back = [weigh_half(1, h, linear[:, 2 * h : 2 * h + 2, :], squared[:, 2 * h : 2 * h + 2, :]) for h in range(2)]
+        own_term(0, whole(sums), "inv_amp11")
         weigh(1, back)
-        neighbour(whole(sums), weighted[0], 0, "inv_amp11")
-        neighbour(whole(sums), weighted[0], 1, "squared11")
-        neighbour(whole(sums), weighted[0], 2)
+        neighbour(whole(sums), weighted[0], 0)
+        neighbour(whole(sums), weighted[0], 1)
+        neighbour(whole(sums), weighted[0], 2, "root00")
         parts = [bank(0, "sums_a", 2), bank(1, "sums_b", 1), bank(2, "sums_c", 1)]
         split = [(parts[0], 0, 0), (parts[0], 1, 1), (parts[1], 0, 2), (parts[2], 0, 3)]
         own_term(1, split, "own_term1")
+        neighbour(split, weighted[1], 0)
         finish(0, sums, 0, TILES, 5)
-        neighbour(split, weighted[1], 0, "scaled0")
-        neighbour(split[:2], weighted[1], 1)
-        neighbour(split[:2], weighted[1], 2, "out_root5")
+        neighbour(split[:2], weighted[1], 1, "scaled0")
+        neighbour(split[:2], weighted[1], 2)
         neighbour(split[2:], weighted[1], 1)
         finish(1, parts[0], 0, 2, 6)
         neighbour(split[2:3], weighted[1], 2)

@@ -39,7 +39,7 @@ def tile_picked_ywmmse_tx_p_kernel(tc, x_words, x_scales, w1, gain, hh, noise, p
 
         xs_all = keep.tile([P, T], U8, name="xs_all")
         nc.gpsimd.memset(xs_all[:].bitcast(I32), 0)
-        ones = keep.tile([P, QUAD], F32, name="ones", tag="inv_amp01", align_bytes=64)
+        ones = keep.tile([P, QUAD], F32, name="ones", tag="words", align_bytes=64)
         nc.gpsimd.memset(ones[:], 1.0)
         count_along = keep.tile([P, QUAD], F32, name="count_along", tag="staged1", align_bytes=64)
         nc.vector.tensor_tensor_scan(count_along[:], ones[:], ones[:], 0.0, ALU.mult, ALU.add)
@@ -67,7 +67,7 @@ def tile_picked_ywmmse_tx_p_kernel(tc, x_words, x_scales, w1, gain, hh, noise, p
             )
         w_rows = w1.rearrange("(p t) n -> p t n", t=PACK)
         w_raw = [keep.tile([P, PACK, P], F32, name="w_raw%d" % b, tag="staged%d" % b, align_bytes=64) for b in range(BLOCKS)]
-        xw_all = keep.tile([P, T], U32, name="xw_all", tag="inv_amp01", align_bytes=64)
+        xw_all = keep.tile([P, T], U32, name="xw_all", tag="words", align_bytes=64)
         nc.sync.dma_start(w_raw[0][:], w_rows[:, :, 0:P])
         nc.sync.dma_start(xw_all[:].bitcast(I32), x_words[0].rearrange("p n t -> p (n t)").bitcast(I32))
         nc.sync.dma_start(w_raw[1][:], w_rows[:, :, P : 2 * P])
@@ -85,8 +85,8 @@ def tile_picked_ywmmse_tx_p_kernel(tc, x_words, x_scales, w1, gain, hh, noise, p
                 grouped[:].rearrange("p (c i) t -> p c t i", i=4),
                 w_raw[b][:].rearrange("p t (c i) -> p c t i", i=4),
             )
-            w_codes.append(keep.tile([P, P], U32, name="w_codes%d" % b, tag=("codes0", "inv_amp01")[b], align_bytes=64))
-            w_scales.append(keep.tile([P, P], U8, name="w_scales%d" % b, tag=("scales0", "inv_amp00")[b], align_bytes=64))
+            w_codes.append(keep.tile([P, P], U32, name="w_codes%d" % b, tag=("codes0", "words")[b], align_bytes=64))
+            w_scales.append(keep.tile([P, P], U8, name="w_scales%d" % b, align_bytes=64))
             nc.vector.quantize_mx(
                 out=w_codes[b][:].bitcast(FP8X4),
                 scales=w_scales[b][:],
@@ -131,14 +131,21 @@ def tile_picked_ywmmse_tx_p_kernel(tc, x_words, x_scales, w1, gain, hh, noise, p
                 out=flat(y), lhsT=w_codes[b][:].bitcast(FP8X4), lhsT_scale=w_scales[b][:],
                 rhs=xw[:, lo:hi].bitcast(FP8X4), rhs_scale=xs[:, lo:hi], start=True, stop=True,
             )
-            nc.scalar.activation(power[b][:, lo:hi], flat(y), ACT.Sigmoid)
+            return y
 
         for half in range(2):
             lo, hi = half * HALF, (half + 1) * HALF
             nc.vector.tensor_copy(xw[:, lo:hi], xw_all[:].indirect(offs_sb[:, lo // 16 : hi // 16]))
-            product(0, 6 + half, lo, hi)
+            nc.scalar.activation(power[0][:, lo:hi], flat(product(0, 6 + half, lo, hi)), ACT.Sigmoid)
         quantise(1, nc.scalar.copy)
-        product(1, 4, 0, S)
+        y = product(1, 4, 0, S)
+        logits = keep.tile([P, S], F32, name="logits", tag="logits", align_bytes=64)
+        nc.scalar.copy(logits[:], flat(y))
+        nc.scalar.activation(power[1][:, :S], flat(y), ACT.Sigmoid)
+        fetched = keep.tile([P, S], F32, name="fetched", tag="fetched", align_bytes=64)
+        for half in range(2):
+            lo, hi = half * HALF, (half + 1) * HALF
+            nc.scalar.activation(fetched[:, lo:hi], logits[:].indirect(pos_sb[0][:, lo // 16 : hi // 16]), ACT.Sigmoid)
 
         turned = bank(5, "turned", 1)
         nc.tensor.transpose(turned[:, 0, :], small[:, :P], ident[:])
@@ -156,19 +163,18 @@ def tile_picked_ywmmse_tx_p_kernel(tc, x_words, x_scales, w1, gain, hh, noise, p
         for t in range(TILES):
             nc.tensor.transpose(own[:, t, :], h_sq[:, t : t + 1].to_broadcast([P, P]), ident[:])
 
-        inv_amp = []
-        for b in range(BLOCKS):
-            power_t = bank((6, 4)[b], "power_t")
+        def inverse_amplitude(b, index, tag):
+            power_t = bank(index, "power_t")
             for t in range(TILES):
                 nc.tensor.transpose(power_t[:, t, :], power[b][:, t * P : (t + 1) * P], ident[:])
-            inv_amp.append([
-                keep.tile([P, 2, P], F32, name="inv_amp%d%d" % (b, h), tag="inv_amp%d%d" % (b, h), align_bytes=64) for h in range(2)
-            ])
+            result = keep.tile([P, TILES, P], F32, name="inv_amp", tag=tag, align_bytes=64)
             for t in range(TILES):
                 nc.scalar.activation(
-                    inv_amp[b][t // 2][:, t % 2, :], power_t[:, t, :], ACT.Abs_reciprocal_sqrt,
-                    bias=1e-30, scale=pri_hh[:, t : t + 1],
+                    result[:, t, :], power_t[:, t, :], ACT.Abs_reciprocal_sqrt, bias=1e-30, scale=pri_hh[:, t : t + 1]
                 )
+            return result
+
+        inv_amp = [inverse_amplitude(0, 6, "logits")]
 
         def neighbour(into, window, d, tag=None):
             lo, hi = into[0][2] * P, (into[-1][2] + 1) * P
@@ -186,7 +192,7 @@ def tile_picked_ywmmse_tx_p_kernel(tc, x_words, x_scales, w1, gain, hh, noise, p
 
         def weigh_half(b, h, linear, squared):
             pair = slice(2 * h, 2 * h + 2)
-            nc.vector.tensor_tensor(scaled[b][:, pair, :], heard[b][h][:], inv_amp[b][h][:], ALU.mult)
+            nc.vector.tensor_tensor(scaled[b][:, pair, :], heard[b][h][:], inv_amp[b][:, pair, :], ALU.mult)
             for i in range(2):
                 nc.scalar.activation(
                     linear[:, i, :], heard[b][h][:, i, :], ACT.Copy, scale=inv_pri[:, 2 * h + i : 2 * h + i + 1]
@@ -232,16 +238,19 @@ def tile_picked_ywmmse_tx_p_kernel(tc, x_words, x_scales, w1, gain, hh, noise, p
         neighbour(first_block, power[0], 1)
         neighbour(first_block[:2], power[0], 2)
         neighbour(first_block[2:], power[0], 2)
+        term = ring.tile([P, S], F32, name="term")
+        nc.vector.tensor_tensor(term[:], fetched[:], gain_sb[0], ALU.mult)
+        add_turned(second_block, lambda t: term[:, t * P : (t + 1) * P], False, False)
+        inv_amp.append(inverse_amplitude(1, 4, "fetched"))
         back = []
         for h in range(2):
             linear = keep.tile([P, 2, P], F32, name="linear", tag="linear%d" % h, align_bytes=64)
             squared = keep.tile([P, 2, P], F32, name="squared", tag="squared%d" % h, align_bytes=64)
             back.append(weigh_half(0, h, linear[:], squared[:]))
-            neighbour(second_block[2 * h : 2 * h + 2], power[1], 0, "inv_amp0%d" % h)
         inv_root = keep.tile([P, TILES], F32, name="inv_root", tag="linear0", align_bytes=64)
         nc.scalar.activation(inv_root[:], pri_hh[:], ACT.Abs_reciprocal_sqrt, bias=1e-30)
         weigh(0, back)
-        neighbour(second_block, power[1], 1, "squared0")
+        neighbour(second_block, power[1], 1, "logits")
         neighbour(second_block[:2], power[1], 2, "squared1")
         neighbour(second_block[2:], power[1], 2)
         sums = bank(4, "sums")
@@ -249,7 +258,7 @@ def tile_picked_ywmmse_tx_p_kernel(tc, x_words, x_scales, w1, gain, hh, noise, p
         linear = keep.tile([P, TILES, P], F32, name="linear", tag="root01", align_bytes=64)
         squared = keep.tile([P, TILES, P], F32, name="squared", tag="root00", align_bytes=64)
         back = [weigh_half(1, h, linear[:, 2 * h : 2 * h + 2, :], squared[:, 2 * h : 2 * h + 2, :]) for h in range(2)]
-        own_term(0, whole(sums), "inv_amp11")
+        own_term(0, whole(sums), "fetched")
         weigh(1, back)
         neighbour(whole(sums), weighted[0], 0)
         neighbour(whole(sums), weighted[0], 1)

from contextlib import ExitStack

import concourse.mybir as mybir

K, T, S, N, D = 512, 2048, 512, 256, 3
P = 128
PACK = 4
BLOCKS = N // P
TILES = S // P
HALF = S // 2
SPARE = 16
QUAD = 32
FLOPS = 2 * K * N * S

F32 = mybir.dt.float32
BF16 = mybir.dt.bfloat16
I32 = mybir.dt.int32
U32 = mybir.dt.uint32
U16 = mybir.dt.uint16
U8 = mybir.dt.uint8
FP8X4 = mybir.dt.float8_e4m3fn_x4
ALU = mybir.AluOpType
ACT = mybir.ActivationFunctionType


def tile_picked_ywmmse_tx_p_kernel(tc, x_words, x_scales, w1, gain, hh, noise, pri, offs, pos1, pos2, pos3, out):
    nc = tc.nc
    with ExitStack() as ctx:
        lists = ctx.enter_context(tc.tile_pool(name="lists", bufs=1))
        keep = ctx.enter_context(tc.tile_pool(name="keep", bufs=1))
        ring = ctx.enter_context(tc.tile_pool(name="ring", bufs=4))
        psum = ctx.enter_context(tc.psum_pool(name="psum", bufs=1))

        def bank(index, name, tiles=TILES):
            return psum.tile([P, tiles, P], F32, name=name, tag="bank%d" % index)

        def flat(tile):
            return tile[:].rearrange("p t c -> p (t c)")

        xs_all = keep.tile([P, T], U8, name="xs_all")
        nc.gpsimd.memset(xs_all[:].bitcast(I32), 0)
        ones = keep.tile([P, QUAD], F32, name="ones", tag="words", align_bytes=64)
        nc.gpsimd.memset(ones[:], 1.0)
        count_along = keep.tile([P, QUAD], F32, name="count_along", tag="staged1", align_bytes=64)
        nc.vector.tensor_tensor_scan(count_along[:], ones[:], ones[:], 0.0, ALU.mult, ALU.add)
        ident = keep.tile([P, P], F32, name="ident")
        nc.vector.memset(ident[:], 0.0)
        count_down = keep.tile([P, QUAD], F32, name="count_down", tag="small", align_bytes=64)
        nc.vector.transpose(count_down[:], count_along[:])
        for q in range(P // QUAD):
            quad = slice(q * QUAD, (q + 1) * QUAD)
            nc.vector.tensor_tensor(ident[quad, quad], count_along[quad, :], count_down[quad, :], ALU.is_equal)
        power = [keep.tile([P, S + SPARE], F32, name="power%d" % b) for b in range(BLOCKS)]
        weighted = [keep.tile([P, S + SPARE], F32, name="weighted%d" % b) for b in range(BLOCKS)]
        for window in power + weighted:
            nc.scalar.activation(window[:, S:], ident[:, :SPARE], ACT.Sigmoid)

        offs_sb = lists.tile([P, S // 16], U16, name="offs_sb")
        pos_sb = [lists.tile([P, S // 16], U16, name="pos_sb%d" % d) for d in range(D)]
        nc.sync.dma_start(offs_sb[:], offs)
        noise_sb = keep.tile([P, BLOCKS, 1], F32, name="noise_sb")
        with nc.allow_non_contiguous_dma(reason="one noise value a partition and block"):
            nc.scalar.dma_start(noise_sb[:], noise.rearrange("(b p) o -> p b o", p=P))
        for q in range(4):
            (nc.sync, nc.scalar)[q % 2].dma_start(
                xs_all[32 * q : 32 * q + 4, :].bitcast(I32), x_scales[0, 4 * q : 4 * q + 4, :].bitcast(I32)
            )
        w_rows = w1.rearrange("(p t) n -> p t n", t=PACK)
        w_raw = [keep.tile([P, PACK, P], F32, name="w_raw%d" % b, tag="staged%d" % b, align_bytes=64) for b in range(BLOCKS)]
        xw_all = keep.tile([P, T], U32, name="xw_all", tag="words", align_bytes=64)
        nc.sync.dma_start(w_raw[0][:], w_rows[:, :, 0:P])
        nc.sync.dma_start(xw_all[:].bitcast(I32), x_words[0].rearrange("p n t -> p (n t)").bitcast(I32))
        nc.sync.dma_start(w_raw[1][:], w_rows[:, :, P : 2 * P])
        small = keep.tile([P, P], F32, name="small", tag="small", align_bytes=64)
        nc.sync.dma_start(small[0:64, :P], hh[0:16, :].rearrange("r (t c) -> (r t) c", c=P))
        nc.sync.dma_start(small[64:128, :P], pri[0:16, :].rearrange("r (t c) -> (r t) c", c=P))
        nc.sync.dma_start(pos_sb[0][:], pos1)

        w_codes = []
        w_scales = []

        def quantise(b, cast):
            grouped = keep.tile([P, P, PACK], BF16, name="grouped%d" % b, tag="grouped%d" % b, align_bytes=64)
            cast(
                grouped[:].rearrange("p (c i) t -> p c t i", i=4),
                w_raw[b][:].rearrange("p t (c i) -> p c t i", i=4),
            )
            w_codes.append(keep.tile([P, P], U32, name="w_codes%d" % b, tag=("codes0", "words")[b], align_bytes=64))
            w_scales.append(keep.tile([P, P], U8, name="w_scales%d" % b, align_bytes=64))
            nc.vector.quantize_mx(
                out=w_codes[b][:].bitcast(FP8X4),
                scales=w_scales[b][:],
                in_=grouped[:].rearrange("p c t -> p (c t)"),
            )

        quantise(0, nc.vector.tensor_copy)
        gain_first = keep.tile([P, S], F32, name="gain_first", tag="staged0", align_bytes=64)
        gain_rest = keep.tile([P, D - 1, S], F32, name="gain_rest", tag="grouped0", align_bytes=64)
        nc.sync.dma_start(gain_first[:], gain[0])
        nc.sync.dma_start(gain_rest[:], gain[1:D].rearrange("d p s -> p d s"))
        nc.sync.dma_start(pos_sb[1][:], pos2)
        nc.sync.dma_start(pos_sb[2][:], pos3)
        gain_sb = [gain_first[:]] + [gain_rest[:, d, :] for d in range(D - 1)]

        xs = keep.tile([P, S], U8, name="xs", align_bytes=64)
        xw = keep.tile([P, S], U32, name="xw", align_bytes=64)
        nc.vector.tensor_copy(xs[:], xs_all[:].indirect(offs_sb[:]))

        def add_turned(into, term, first, last):
            for place, (target, slot, t) in enumerate(into):
                opens = place == 0 or into[place - 1][0] is not target
                closes = place == len(into) - 1 or into[place + 1][0] is not target
                nc.tensor.matmul(
                    target[:, slot, :], term(t), ident[:], is_transpose=True,
                    start=first and opens, stop=last and closes,
                )

        def whole(target):
            return [(target, t, t) for t in range(TILES)]

        def halves(banks):
            return [(banks[t // 2], t % 2, t) for t in range(TILES)]

        heard = [[bank(2 * b + h, "heard", 2) for h in range(2)] for b in range(BLOCKS)]
        for b in range(BLOCKS):
            add_turned(halves(heard[b]), lambda t: noise_sb[:, b, :].to_broadcast([P, P]), True, False)

        def product(b, index, lo, hi):
            y = bank(index, "y", (hi - lo) // P)
            nc.tensor.matmul_mx(
                out=flat(y), lhsT=w_codes[b][:].bitcast(FP8X4), lhsT_scale=w_scales[b][:],
                rhs=xw[:, lo:hi].bitcast(FP8X4), rhs_scale=xs[:, lo:hi], start=True, stop=True,
            )
            return y

        for half in range(2):
            lo, hi = half * HALF, (half + 1) * HALF
            nc.vector.tensor_copy(xw[:, lo:hi], xw_all[:].indirect(offs_sb[:, lo // 16 : hi // 16]))
            nc.scalar.activation(power[0][:, lo:hi], flat(product(0, 6 + half, lo, hi)), ACT.Sigmoid)
        quantise(1, nc.scalar.copy)
        y = product(1, 4, 0, S)
        logits = keep.tile([P, S], F32, name="logits", tag="logits", align_bytes=64)
        nc.scalar.copy(logits[:], flat(y))
        nc.scalar.activation(power[1][:, :S], flat(y), ACT.Sigmoid)
        fetched = keep.tile([P, S], F32, name="fetched", tag="fetched", align_bytes=64)
        for half in range(2):
            lo, hi = half * HALF, (half + 1) * HALF
            nc.scalar.activation(fetched[:, lo:hi], logits[:].indirect(pos_sb[0][:, lo // 16 : hi // 16]), ACT.Sigmoid)

        turned = bank(5, "turned", 1)
        nc.tensor.transpose(turned[:, 0, :], small[:, :P], ident[:])
        cols = keep.tile([P, 2, TILES], F32, name="cols", tag="grouped1", align_bytes=64)
        nc.vector.tensor_copy(cols[:], turned[:, 0, :].rearrange("p (a r) -> p a r", a=2)[:, :, 0:TILES])
        h_sq = keep.tile([P, TILES], F32, name="h_sq")
        nc.vector.tensor_tensor(h_sq[:], cols[:, 0, :], cols[:, 0, :], ALU.mult)
        pri_pos = keep.tile([P, TILES], F32, name="pri_pos")
        nc.vector.tensor_scalar(pri_pos[:], cols[:, 1, :], 1e-30, None, ALU.max)
        pri_hh = keep.tile([P, TILES], F32, name="pri_hh")
        nc.vector.tensor_tensor(pri_hh[:], h_sq[:], cols[:, 1, :], ALU.mult)
        inv_pri = keep.tile([P, TILES], F32, name="inv_pri")
        nc.vector.reciprocal(inv_pri[:], pri_pos[:])
        own = bank(7, "own")
        for t in range(TILES):
            nc.tensor.transpose(own[:, t, :], h_sq[:, t : t + 1].to_broadcast([P, P]), ident[:])

        def inverse_amplitude(b, index, tag):
            power_t = bank(index, "power_t")
            for t in range(TILES):
                nc.tensor.transpose(power_t[:, t, :], power[b][:, t * P : (t + 1) * P], ident[:])
            result = keep.tile([P, TILES, P], F32, name="inv_amp", tag=tag, align_bytes=64)
            for t in range(TILES):
                nc.scalar.activation(
                    result[:, t, :], power_t[:, t, :], ACT.Abs_reciprocal_sqrt, bias=1e-30, scale=pri_hh[:, t : t + 1]
                )
            return result

        inv_amp = [inverse_amplitude(0, 6, "logits")]

        def neighbour(into, window, d, tag=None):
            lo, hi = into[0][2] * P, (into[-1][2] + 1) * P
            if tag is None:
                term = ring.tile([P, hi - lo], F32, name="term")
            else:
                term = keep.tile([P, hi - lo], F32, name="term", tag=tag, align_bytes=64)
            nc.vector.tensor_tensor(
                term[:], window[:].indirect(pos_sb[d][:, lo // 16 : hi // 16]), gain_sb[d][:, lo:hi], ALU.mult
            )
            add_turned(into, lambda t: term[:, t * P - lo : (t + 1) * P - lo], False, d == D - 1)

        scaled = [keep.tile([P, TILES, P], F32, name="scaled0", tag="scaled0", align_bytes=64)]


        def weigh_half(b, h, linear, squared):
            pair = slice(2 * h, 2 * h + 2)
            nc.vector.tensor_tensor(scaled[b][:, pair, :], heard[b][h][:], inv_amp[b][:, pair, :], ALU.mult)
            for i in range(2):
                nc.scalar.activation(
                    linear[:, i, :], heard[b][h][:, i, :], ACT.Copy, scale=inv_pri[:, 2 * h + i : 2 * h + i + 1]
                )
            nc.scalar.activation(squared, scaled[b][:, pair, :], ACT.Square)
            back = bank(5 + h, "back", 2)
            into = [(back, i, i) for i in range(2)]
            add_turned(into, lambda i: linear[:, i, :], True, False)
            add_turned(into, lambda i: squared[:, i, :], False, True)
            return back

        def weigh(b, back):
            root = [keep.tile([P, HALF], F32, name="root", tag="root%d%d" % (b, h), align_bytes=64) for h in range(2)]
            for h in range(2):
                nc.scalar.activation(root[h][:], flat(back[h]), ACT.Abs_reciprocal_sqrt)
            for h in range(2):
                nc.scalar.activation(weighted[b][:, h * HALF : (h + 1) * HALF], root[h][:], ACT.Square)

        def own_term(b, into, tag):
            term = keep.tile([P, S], F32, name="own_term", tag=tag, align_bytes=64)
            nc.vector.tensor_tensor(term[:], weighted[b][:, :S], flat(own), ALU.mult)
            add_turned(into, lambda t: term[:, t * P : (t + 1) * P], True, False)

        def finish(b, sums, first, count, index):
            denom = keep.tile([P, count, P], F32, name="denom%d" % index)
            nc.vector.scalar_tensor_tensor(
                denom[:], sums[:], 0.3, scaled[b][:, first : first + count, :], ALU.add, ALU.mult
            )
            out_root = keep.tile([P, count, P], F32, name="out_root", tag="out_root%d" % index, align_bytes=64)
            back = bank(index, "back_out", count)
            for t in range(count):
                nc.scalar.activation(
                    out_root[:, t, :], denom[:, t, :], ACT.Abs_reciprocal_sqrt,
                    scale=inv_root[:, first + t : first + t + 1],
                )
                nc.tensor.transpose(back[:, t, :], out_root[:, t, :], ident[:])
            result = keep.tile([P, count * P], F32, name="result%d" % index)
            nc.scalar.activation(result[:], flat(back), ACT.Square)
            nc.sync.dma_start(out[b * P : (b + 1) * P, first * P : (first + count) * P], result[:])

        first_block, second_block = halves(heard[0]), halves(heard[1])
        neighbour(first_block, power[0], 0)
        neighbour(first_block, power[0], 1)
        neighbour(first_block[:2], power[0], 2)
        neighbour(first_block[2:], power[0], 2)
        term = ring.tile([P, S], F32, name="term")
        nc.vector.tensor_tensor(term[:], fetched[:], gain_sb[0], ALU.mult)
        add_turned(second_block, lambda t: term[:, t * P : (t + 1) * P], False, False)
        inv_amp.append(inverse_amplitude(1, 4, "fetched"))
        back = []
        for h in range(2):
            linear = keep.tile([P, 2, P], F32, name="linear", tag="linear%d" % h, align_bytes=64)
            squared = keep.tile([P, 2, P], F32, name="squared", tag="squared%d" % h, align_bytes=64)
            back.append(weigh_half(0, h, linear[:], squared[:]))
        inv_root = keep.tile([P, TILES], F32, name="inv_root", tag="linear0", align_bytes=64)
        nc.scalar.activation(inv_root[:], pri_hh[:], ACT.Abs_reciprocal_sqrt, bias=1e-30)
        weigh(0, back)
        neighbour(second_block, power[1], 1, "logits")
        neighbour(second_block[:2], power[1], 2, "squared1")
        neighbour(second_block[2:], power[1], 2)
        sums = bank(4, "sums")
        scaled.append(keep.tile([P, TILES, P], F32, name="scaled1", tag="scaled1", align_bytes=64))
        linear = keep.tile([P, TILES, P], F32, name="linear", tag="root01", align_bytes=64)
        squared = keep.tile([P, TILES, P], F32, name="squared", tag="root00", align_bytes=64)
        back = [weigh_half(1, h, linear[:, 2 * h : 2 * h + 2, :], squared[:, 2 * h : 2 * h + 2, :]) for h in range(2)]
        own_term(0, whole(sums), "fetched")
        weigh(1, back)
        neighbour(whole(sums), weighted[0], 0)
        neighbour(whole(sums), weighted[0], 1)
        neighbour(whole(sums), weighted[0], 2, "root00")
        parts = [bank(0, "sums_a", 2), bank(1, "sums_b", 1), bank(2, "sums_c", 1)]
        split = [(parts[0], 0, 0), (parts[0], 1, 1), (parts[1], 0, 2), (parts[2], 0, 3)]
        own_term(1, split, "own_term1")
        neighbour(split, weighted[1], 0)
        finish(0, sums, 0, TILES, 5)
        neighbour(split[:2], weighted[1], 1, "scaled0")
        neighbour(split[:2], weighted[1], 2)
        neighbour(split[2:], weighted[1], 1)
        finish(1, parts[0], 0, 2, 6)
        neighbour(split[2:3], weighted[1], 2)
        neighbour(split[3:], weighted[1], 2)
        finish(1, parts[1], 2, 1, 3)
        finish(1, parts[2], 3, 1, 4)
